import numpy as np
import ml_dtypes


def mxq(x, axis, fmt="e4m3"):
    dtype, down = {"e4m3": (ml_dtypes.float8_e4m3fn, 7), "e5m2": (ml_dtypes.float8_e5m2, 14)}[fmt]
    v = np.moveaxis(np.asarray(x, np.float32).astype(ml_dtypes.bfloat16).astype(np.float64), axis, -1)
    blocks = v.reshape(v.shape[:-1] + (-1, 32))
    amax = np.abs(blocks).max(-1, keepdims=True)
    byte = np.maximum(np.where(amax > 0, np.frexp(amax)[1] - 1 + 127, 0) - down, 1)
    scale = np.exp2(byte - 127.0)
    codes = (blocks / scale).astype(np.float32).astype(dtype).astype(np.float64)
    return np.moveaxis((codes * scale).reshape(v.shape), -1, axis)


WIDE = False


def mx_kscale(k):
    if not WIDE:
        return np.ones(k)
    levels = np.array([10, -10, 5, -5, 0])
    if k % 512:
        return np.exp2(np.random.permutation(np.resize(levels, k // 32))).repeat(32)
    a = np.empty((k // 512, 16))
    for p in range(k // 512):
        a[p, :8] = np.random.permutation(np.resize(levels, 8))
        for g in range(8):
            far = levels[np.abs(levels - a[p, g]) >= 10]
            a[p, g + 8] = far[np.random.randint(len(far))]
    return np.exp2(a.ravel()).repeat(32)


def f64(x):
    return np.asarray(x).astype(np.float64)


def striped(idx):
    return np.tile(idx.reshape(-1, 16).T, (8, 1)).astype(np.uint16)


def unstriped(offs):
    return offs[:16].T.reshape(-1).astype(np.int64)


E2M1 = np.array([0.0, 0.5, 1.0, 1.5, 2.0, 3.0, 4.0, 6.0, -0.0, -0.5, -1.0, -1.5, -2.0, -3.0, -4.0, -6.0])


def pack_weight(w, fmt):
    k, n = w.shape
    w = f64(np.asarray(w, np.float32).astype(ml_dtypes.bfloat16)).reshape(k // 32, 32, n)
    amax = np.abs(w).max(1)
    if fmt == "e4m3":
        byte = np.frexp(amax)[1] - 1 + 127 - 7
    else:
        mant, ex = np.frexp(amax / 6.0)
        byte = np.where(mant > 0.5, ex, ex - 1) + 127
    byte = np.clip(np.where(amax > 0, byte, 1), 1, 254)
    scaled = (w * np.exp2(127.0 - byte)[:, None, :]).reshape(k, n).astype(np.float32)
    by_word = np.ascontiguousarray(scaled.reshape(k // 512, 128, 4, n).transpose(0, 1, 3, 2))
    if fmt == "e4m3":
        words = by_word.astype(ml_dtypes.float8_e4m3fn).view(np.uint8)
    else:
        c = by_word.astype(ml_dtypes.float4_e2m1fn).view(np.uint8) & 0xF
        words = (c[..., 0::2] | (c[..., 1::2] << 4)).reshape(k // 512, 128, 2 * n)
    return np.ascontiguousarray(words), np.ascontiguousarray(byte.astype(np.uint8).reshape(k // 512, 16, n))


def unpack_weight(words, scales, fmt):
    g, _, n = scales.shape
    words = np.ascontiguousarray(words).reshape(g, 128, n, -1)
    if fmt == "e4m3":
        vals = words.view(ml_dtypes.float8_e4m3fn).astype(np.float64)
    else:
        nib = np.empty((g, 128, n, 4), np.uint8)
        nib[..., 0::2] = words & 0xF
        nib[..., 1::2] = words >> 4
        vals = E2M1[nib]
    vals = vals * np.repeat(np.exp2(scales.astype(np.float64) - 127.0), 8, axis=1)[..., None]
    return vals.transpose(0, 1, 3, 2).reshape(g * 512, n)


K, T, E, C, N = 1024, 1280, 6, 128, 256


def by_expert(wq, xq):
    return np.concatenate([wq[e].T @ xq[:, e * C:(e + 1) * C] for e in range(E)], axis=1)


def setup_inputs():
    n = np.random.standard_normal
    s = mx_kscale(K)[:, None]
    w = [pack_weight(m, "e2m1") for m in n((E, K, N)) / np.sqrt(K) / s[None]]
    return {
        "xT": (n((K, T)) * s).astype(np.float32),
        "xr": n((N, T)).astype(np.float32),
        "w_words": np.stack([m[0] for m in w]),
        "w_scales": np.stack([m[1] for m in w]),
        "b": (0.3 * n((N, E))).astype(np.float32),
        "gate": np.tile(np.random.uniform(0.2, 1.0, E * C), (N, 1)).astype(np.float32),
        "offs": striped(np.random.permutation(T)[:E * C]),
    }


def reference(xT, xr, w_words, w_scales, b, gate, offs):
    idx = unstriped(offs)
    w = np.stack([unpack_weight(w_words[e], w_scales[e], "e2m1") for e in range(E)])
    xq = mxq(f64(xT)[:, idx], 0, "e4m3")
    y = by_expert(w, xq)
    y = y + np.repeat(f64(b), C, axis=1)
    out = f64(xr).copy()
    out[:, idx] += f64(gate) * y
    return out

@@ -1,0 +1,163 @@
+from contextlib import ExitStack
+
+import concourse.mybir as mybir
+
+K, T, E, C, N = 1024, 1280, 6, 128, 256
+S = E * C
+P = 128
+K_PASS = 512
+PASSES = K // K_PASS
+HALVES = N // P
+
+FLOPS = 2 * S * K * N
+BYTES = 4 * K * T + 8 * N * T + E * K * N // 2 + E * K * N // 32 + 4 * N * E + 4 * S + 2 * P * S // 16
+
+F32 = mybir.dt.float32
+BF16 = mybir.dt.bfloat16
+I32 = mybir.dt.int32
+U32 = mybir.dt.uint32
+U16 = mybir.dt.uint16
+U8 = mybir.dt.uint8
+FP8X4 = mybir.dt.float8_e4m3fn_x4
+FP4X4 = mybir.dt.float4_e2m1fn_x4
+ADD, MULT = mybir.AluOpType.add, mybir.AluOpType.mult
+COPY = mybir.ActivationFunctionType.Copy
+
+CHUNKS = (
+    ((0, 256, 192), (256, 512, 400), (768, 512, 400)),
+    ((0, 512, 400), (512, 512, 384), (1024, 256, 96)),
+)
+PIECE = 2
+
+
+def interleave(ap_in, ap_out):
+    src = ap_in.rearrange("p j (c i) -> p c j i", i=4)
+    dst = ap_out.rearrange("p (c i) j -> p c j i", i=4)
+    return dst, src
+
+
+def tile_moe_res_lin_bias_kernel(tc, xT, xr, w_words, w_scales, b, gate, offs, out):
+    nc = tc.nc
+    with ExitStack() as ctx:
+        keep = ctx.enter_context(tc.tile_pool(name="keep", bufs=1))
+        psum = ctx.enter_context(tc.psum_pool(name="psum", bufs=1))
+
+        offsets = keep.tile([P, S // 16], U16, name="offsets")
+        nc.sync.dma_start(offsets[:], offs)
+
+        words = [keep.tile([P, T], U32, name=f"words{a}", align_bytes=64) for a in range(PASSES)]
+        scales = [keep.tile([P, T], U8, name=f"scales{a}", align_bytes=64) for a in range(PASSES)]
+        slot_words = [keep.tile([P, S], U32, name=f"slot_words{a}", align_bytes=64) for a in range(PASSES)]
+        slot_scales = [keep.tile([P, S], U8, name=f"slot_scales{a}", align_bytes=64) for a in range(PASSES)]
+        w_code = keep.tile([P, E * PASSES, 2 * N], U8, name="w_code", align_bytes=64)
+        w_scale = keep.tile([P, E * PASSES * N], U8, name="w_scale", align_bytes=64)
+        window = [keep.tile([P, T], F32, name=f"window{h}") for h in range(HALVES)]
+        result = [keep.tile([P, S], F32, name=f"result{h}") for h in range(HALVES)]
+        total = [keep.tile([P, T], F32, name=f"total{h}") for h in range(HALVES)]
+        residual = [keep.tile([P, T], F32, name=f"residual{h}") for h in range(HALVES)]
+        bias = keep.tile([P, HALVES, 8], F32, name="bias")
+        gates = keep.tile([P, S], F32, name="gates")
+
+        nc.gpsimd.memset(scales[0][:].bitcast(I32), 0)
+        nc.gpsimd.memset(scales[1][:].bitcast(I32), 0)
+        nc.gpsimd.memset(w_scale[:].bitcast(I32), 0)
+        for h in range(HALVES):
+            nc.gpsimd.memset(window[h][:], 0.0)
+
+        raws = []
+        for a in range(PASSES):
+            row = []
+            for i, (t0, width, on_scalar) in enumerate(CHUNKS[a]):
+                raw = keep.tile([P, 4, width], F32, name=f"raw{a}_{i}")
+                nc.sync.dma_start(
+                    raw[:], xT[a * K_PASS : (a + 1) * K_PASS, t0 : t0 + width].rearrange("(p j) w -> p j w", j=4)
+                )
+                row.append(raw)
+            raws.append(row)
+
+        w_scale_words = w_scale[:].bitcast(I32).rearrange("p (g n) -> p g n", g=E * PASSES)
+        scale_rows = w_scales.bitcast(I32).rearrange("e a q n -> q (e a) n")
+        for quadrant in range(4):
+            nc.sync.dma_start(
+                w_scale_words[32 * quadrant : 32 * quadrant + 4], scale_rows[4 * quadrant : 4 * quadrant + 4]
+            )
+        code_rows = w_words.rearrange("e a p n -> p (e a) n")
+        for e0 in range(0, E, PIECE):
+            g = slice(e0 * PASSES, (e0 + PIECE) * PASSES)
+            nc.sync.dma_start(w_code[:, g, :], code_rows[:, g, :])
+        nc.sync.dma_start(bias[:, :, 0:E], b.rearrange("(h p) e -> p h e", p=P))
+        nc.sync.dma_start(gates[:], gate[0:P, :])
+        for h in range(HALVES):
+            nc.sync.dma_start(residual[h][:], xr[h * P : (h + 1) * P, :])
+
+        for a in range(PASSES):
+            for i, (t0, width, on_scalar) in enumerate(CHUNKS[a]):
+                raw = raws[a][i]
+                grouped = keep.tile([P, width, 4], BF16, name=f"grouped{a}_{i}", align_bytes=64)
+                dst, src = interleave(raw[:, :, 0:on_scalar], grouped[:, 0:on_scalar, :])
+                nc.scalar.activation(dst, src, COPY)
+                dst, src = interleave(raw[:, :, on_scalar:width], grouped[:, on_scalar:width, :])
+                nc.vector.tensor_copy(dst, src)
+                nc.vector.quantize_mx(
+                    out=words[a][:, t0 : t0 + width].bitcast(FP8X4),
+                    scales=scales[a][:, t0 : t0 + width],
+                    in_=grouped[:].rearrange("p w j -> p (w j)"),
+                )
+            if a == 0:
+                nc.vector.tensor_copy(slot_words[a][:], words[a][:].indirect(offsets[:]))
+                nc.vector.tensor_copy(slot_scales[a][:], scales[a][:].indirect(offsets[:]))
+
+        banks = [
+            [psum.tile([P, PIECE * C], F32, name=f"bank{h}_{i}") for i in range(E // PIECE)] for h in range(HALVES)
+        ]
+
+        def multiply(h, i):
+            for e in range(i * PIECE, (i + 1) * PIECE):
+                slots = slice(e * C, (e + 1) * C)
+                local = slice((e - i * PIECE) * C, (e - i * PIECE + 1) * C)
+                for a in range(PASSES):
+                    g = e * PASSES + a
+                    nc.tensor.matmul_mx(
+                        out=banks[h][i][:, local],
+                        lhsT=w_code[:, g, 2 * P * h : 2 * P * (h + 1)].bitcast(FP4X4),
+                        lhsT_scale=w_scale[:, g * N + h * P : g * N + (h + 1) * P],
+                        rhs=slot_words[a][:, slots].bitcast(FP8X4),
+                        rhs_scale=slot_scales[a][:, slots],
+                        start=(a == 0),
+                        stop=(a == PASSES - 1),
+                    )
+
+        def leave_bank(h, i):
+            for e in range(i * PIECE, (i + 1) * PIECE):
+                slots = slice(e * C, (e + 1) * C)
+                local = slice((e - i * PIECE) * C, (e - i * PIECE + 1) * C)
+                nc.vector.scalar_tensor_tensor(
+                    out=result[h][:, slots],
+                    in0=banks[h][i][:, local],
+                    scalar=bias[:, h, e : e + 1],
+                    in1=gates[:, slots],
+                    op0=ADD,
+                    op1=MULT,
+                )
+
+        a = PASSES - 1
+        for i in range(E // PIECE):
+            slots = slice(i * PIECE * C, (i + 1) * PIECE * C)
+            part = slice(i * PIECE * C // 16, (i + 1) * PIECE * C // 16)
+            nc.vector.tensor_copy(slot_words[a][:, slots], words[a][:].indirect(offsets[:, part]))
+            nc.vector.tensor_copy(slot_scales[a][:, slots], scales[a][:].indirect(offsets[:, part]))
+            multiply(0, i)
+        for i in range(E // PIECE):
+            multiply(1, i)
+        for i in range(E // PIECE):
+            leave_bank(0, i)
+        leave_bank(1, 0)
+        nc.vector.tensor_copy(window[0][:].indirect(offsets[:]), result[0][:])
+        leave_bank(1, 1)
+        leave_bank(1, 2)
+        nc.vector.tensor_tensor(total[0][:], window[0][:], residual[0][:], ADD)
+        nc.sync.dma_start(out[0:P, :], total[0][:])
+        nc.vector.tensor_copy(window[1][:].indirect(offsets[:]), result[1][:])
+        for t0, t1 in ((0, 768), (768, T)):
+            nc.vector.tensor_tensor(total[1][:, t0:t1], window[1][:, t0:t1], residual[1][:, t0:t1], ADD)
+            nc.sync.dma_start(out[P:N, t0:t1], total[1][:, t0:t1])

@@ -21,11 +21,11 @@ U8 = mybir.dt.uint8
 FP8X4 = mybir.dt.float8_e4m3fn_x4
 FP4X4 = mybir.dt.float4_e2m1fn_x4
 ADD, MULT = mybir.AluOpType.add, mybir.AluOpType.mult
-COPY = mybir.ActivationFunctionType.Copy
+IDENTITY = mybir.ActivationFunctionType.Identity
 
 CHUNKS = (
-    ((0, 256, 192), (256, 512, 400), (768, 512, 400)),
-    ((0, 512, 400), (512, 512, 384), (1024, 256, 96)),
+    ((0, 512, 184), (512, 512, 184), (1024, 256, 96)),
+    ((0, 256, 256), (256, 512, 432), (768, 256, 160), (1024, 256, 80)),
 )
 PIECE = 2
 
@@ -43,7 +43,6 @@ def tile_moe_res_lin_bias_kernel(tc, xT, xr, w_words, w_scales, b, gate, offs, o
         psum = ctx.enter_context(tc.psum_pool(name="psum", bufs=1))
 
         offsets = keep.tile([P, S // 16], U16, name="offsets")
-        nc.sync.dma_start(offsets[:], offs)
 
         words = [keep.tile([P, T], U32, name=f"words{a}", align_bytes=64) for a in range(PASSES)]
         scales = [keep.tile([P, T], U8, name=f"scales{a}", align_bytes=64) for a in range(PASSES)]
@@ -62,7 +61,7 @@ def tile_moe_res_lin_bias_kernel(tc, xT, xr, w_words, w_scales, b, gate, offs, o
         nc.gpsimd.memset(scales[1][:].bitcast(I32), 0)
         nc.gpsimd.memset(w_scale[:].bitcast(I32), 0)
         for h in range(HALVES):
-            nc.gpsimd.memset(window[h][:], 0.0)
+            nc.vector.memset(window[h][:], 0.0)
 
         raws = []
         for a in range(PASSES):
@@ -73,6 +72,8 @@ def tile_moe_res_lin_bias_kernel(tc, xT, xr, w_words, w_scales, b, gate, offs, o
                     raw[:], xT[a * K_PASS : (a + 1) * K_PASS, t0 : t0 + width].rearrange("(p j) w -> p j w", j=4)
                 )
                 row.append(raw)
+                if a == 0 and i == 0:
+                    nc.sync.dma_start(offsets[:], offs)
             raws.append(row)
 
         w_scale_words = w_scale[:].bitcast(I32).rearrange("p (g n) -> p g n", g=E * PASSES)
@@ -81,11 +82,11 @@ def tile_moe_res_lin_bias_kernel(tc, xT, xr, w_words, w_scales, b, gate, offs, o
             nc.sync.dma_start(
                 w_scale_words[32 * quadrant : 32 * quadrant + 4], scale_rows[4 * quadrant : 4 * quadrant + 4]
             )
+        nc.sync.dma_start(bias[:, :, 0:E], b.rearrange("(h p) e -> p h e", p=P))
         code_rows = w_words.rearrange("e a p n -> p (e a) n")
         for e0 in range(0, E, PIECE):
             g = slice(e0 * PASSES, (e0 + PIECE) * PASSES)
             nc.sync.dma_start(w_code[:, g, :], code_rows[:, g, :])
-        nc.sync.dma_start(bias[:, :, 0:E], b.rearrange("(h p) e -> p h e", p=P))
         nc.sync.dma_start(gates[:], gate[0:P, :])
         for h in range(HALVES):
             nc.sync.dma_start(residual[h][:], xr[h * P : (h + 1) * P, :])
@@ -95,9 +96,10 @@ def tile_moe_res_lin_bias_kernel(tc, xT, xr, w_words, w_scales, b, gate, offs, o
                 raw = raws[a][i]
                 grouped = keep.tile([P, width, 4], BF16, name=f"grouped{a}_{i}", align_bytes=64)
                 dst, src = interleave(raw[:, :, 0:on_scalar], grouped[:, 0:on_scalar, :])
-                nc.scalar.activation(dst, src, COPY)
-                dst, src = interleave(raw[:, :, on_scalar:width], grouped[:, on_scalar:width, :])
-                nc.vector.tensor_copy(dst, src)
+                nc.scalar.activation(dst, src, IDENTITY)
+                if on_scalar < width:
+                    dst, src = interleave(raw[:, :, on_scalar:width], grouped[:, on_scalar:width, :])
+                    nc.vector.tensor_copy(dst, src)
                 nc.vector.quantize_mx(
                     out=words[a][:, t0 : t0 + width].bitcast(FP8X4),
                     scales=scales[a][:, t0 : t0 + width],
@@ -131,14 +133,19 @@ def tile_moe_res_lin_bias_kernel(tc, xT, xr, w_words, w_scales, b, gate, offs, o
             for e in range(i * PIECE, (i + 1) * PIECE):
                 slots = slice(e * C, (e + 1) * C)
                 local = slice((e - i * PIECE) * C, (e - i * PIECE + 1) * C)
-                nc.vector.scalar_tensor_tensor(
-                    out=result[h][:, slots],
-                    in0=banks[h][i][:, local],
-                    scalar=bias[:, h, e : e + 1],
-                    in1=gates[:, slots],
-                    op0=ADD,
-                    op1=MULT,
-                )
+                nc.scalar.activation(result[h][:, slots], banks[h][i][:, local], IDENTITY, bias=bias[:, h, e : e + 1])
+
+        def scatter(h, i):
+            slots = slice(i * PIECE * C, (i + 1) * PIECE * C)
+            part = slice(i * PIECE * C // 16, (i + 1) * PIECE * C // 16)
+            nc.vector.tensor_tensor(
+                window[h][:].indirect(offsets[:, part]), result[h][:, slots], gates[:, slots], MULT
+            )
+
+        def finish(h, cuts):
+            for t0, t1 in cuts:
+                nc.vector.tensor_tensor(total[h][:, t0:t1], window[h][:, t0:t1], residual[h][:, t0:t1], ADD)
+                nc.sync.dma_start(out[h * P : (h + 1) * P, t0:t1], total[h][:, t0:t1])
 
         a = PASSES - 1
         for i in range(E // PIECE):
@@ -146,18 +153,14 @@ def tile_moe_res_lin_bias_kernel(tc, xT, xr, w_words, w_scales, b, gate, offs, o
             part = slice(i * PIECE * C // 16, (i + 1) * PIECE * C // 16)
             nc.vector.tensor_copy(slot_words[a][:, slots], words[a][:].indirect(offsets[:, part]))
             nc.vector.tensor_copy(slot_scales[a][:, slots], scales[a][:].indirect(offsets[:, part]))
-            multiply(0, i)
-        for i in range(E // PIECE):
-            multiply(1, i)
-        for i in range(E // PIECE):
-            leave_bank(0, i)
-        leave_bank(1, 0)
-        nc.vector.tensor_copy(window[0][:].indirect(offsets[:]), result[0][:])
-        leave_bank(1, 1)
-        leave_bank(1, 2)
-        nc.vector.tensor_tensor(total[0][:], window[0][:], residual[0][:], ADD)
-        nc.sync.dma_start(out[0:P, :], total[0][:])
-        nc.vector.tensor_copy(window[1][:].indirect(offsets[:]), result[1][:])
-        for t0, t1 in ((0, 768), (768, T)):
-            nc.vector.tensor_tensor(total[1][:, t0:t1], window[1][:, t0:t1], residual[1][:, t0:t1], ADD)
-            nc.sync.dma_start(out[P:N, t0:t1], total[1][:, t0:t1])
+        for h, i in ((0, 0), (0, 1), (1, 0), (0, 2), (1, 1), (1, 2)):
+            multiply(h, i)
+            leave_bank(h, i)
+        scatter(0, 0)
+        scatter(0, 1)
+        scatter(1, 0)
+        scatter(0, 2)
+        scatter(1, 1)
+        finish(0, ((0, T),))
+        scatter(1, 2)
+        finish(1, ((0, 768), (768, T)))

@@ -25,7 +25,7 @@ IDENTITY = mybir.ActivationFunctionType.Identity
 
 CHUNKS = (
     ((0, 512, 184), (512, 512, 184), (1024, 256, 96)),
-    ((0, 256, 256), (256, 512, 432), (768, 256, 160), (1024, 256, 80)),
+    ((0, 256, 256), (256, 512, 448), (768, 256, 192), (1024, 256, 96)),
 )
 PIECE = 2
 
@@ -52,6 +52,7 @@ def tile_moe_res_lin_bias_kernel(tc, xT, xr, w_words, w_scales, b, gate, offs, o
         w_scale = keep.tile([P, E * PASSES * N], U8, name="w_scale", align_bytes=64)
         window = [keep.tile([P, T], F32, name=f"window{h}") for h in range(HALVES)]
         result = [keep.tile([P, S], F32, name=f"result{h}") for h in range(HALVES)]
+        scaled = [keep.tile([P, S], F32, name=f"scaled{h}") for h in range(HALVES)]
         total = [keep.tile([P, T], F32, name=f"total{h}") for h in range(HALVES)]
         residual = [keep.tile([P, T], F32, name=f"residual{h}") for h in range(HALVES)]
         bias = keep.tile([P, HALVES, 8], F32, name="bias")
@@ -77,17 +78,16 @@ def tile_moe_res_lin_bias_kernel(tc, xT, xr, w_words, w_scales, b, gate, offs, o
             raws.append(row)
 
         w_scale_words = w_scale[:].bitcast(I32).rearrange("p (g n) -> p g n", g=E * PASSES)
-        scale_rows = w_scales.bitcast(I32).rearrange("e a q n -> q (e a) n")
-        for quadrant in range(4):
-            nc.sync.dma_start(
-                w_scale_words[32 * quadrant : 32 * quadrant + 4], scale_rows[4 * quadrant : 4 * quadrant + 4]
-            )
-        nc.sync.dma_start(bias[:, :, 0:E], b.rearrange("(h p) e -> p h e", p=P))
+        scale_rows = w_scales.bitcast(I32).rearrange("e a (q r) n -> r q (e a) n", r=4)
+        for r in range(4):
+            nc.sync.dma_start(w_scale_words[r:P:32], scale_rows[r])
         code_rows = w_words.rearrange("e a p n -> p (e a) n")
         for e0 in range(0, E, PIECE):
             g = slice(e0 * PASSES, (e0 + PIECE) * PASSES)
             nc.sync.dma_start(w_code[:, g, :], code_rows[:, g, :])
-        nc.sync.dma_start(gates[:], gate[0:P, :])
+            if e0 == 0:
+                nc.sync.dma_start(bias[:, :, 0:E], b.rearrange("(h p) e -> p h e", p=P))
+                nc.sync.dma_start(gates[:], gate[0:P, :])
         for h in range(HALVES):
             nc.sync.dma_start(residual[h][:], xr[h * P : (h + 1) * P, :])
 
@@ -100,11 +100,16 @@ def tile_moe_res_lin_bias_kernel(tc, xT, xr, w_words, w_scales, b, gate, offs, o
                 if on_scalar < width:
                     dst, src = interleave(raw[:, :, on_scalar:width], grouped[:, on_scalar:width, :])
                     nc.vector.tensor_copy(dst, src)
-                nc.vector.quantize_mx(
-                    out=words[a][:, t0 : t0 + width].bitcast(FP8X4),
-                    scales=scales[a][:, t0 : t0 + width],
-                    in_=grouped[:].rearrange("p w j -> p (w j)"),
-                )
+                flat = grouped[:].rearrange("p w j -> p (w j)")
+                done = 0
+                while done < width:
+                    cut = max(n for n in (512, 256, 128) if n <= width - done)
+                    nc.vector.quantize_mx(
+                        out=words[a][:, t0 + done : t0 + done + cut].bitcast(FP8X4),
+                        scales=scales[a][:, t0 + done : t0 + done + cut],
+                        in_=flat[:, 4 * done : 4 * (done + cut)],
+                    )
+                    done += cut
             if a == 0:
                 nc.vector.tensor_copy(slot_words[a][:], words[a][:].indirect(offsets[:]))
                 nc.vector.tensor_copy(slot_scales[a][:], scales[a][:].indirect(offsets[:]))
@@ -135,32 +140,31 @@ def tile_moe_res_lin_bias_kernel(tc, xT, xr, w_words, w_scales, b, gate, offs, o
                 local = slice((e - i * PIECE) * C, (e - i * PIECE + 1) * C)
                 nc.scalar.activation(result[h][:, slots], banks[h][i][:, local], IDENTITY, bias=bias[:, h, e : e + 1])
 
-        def scatter(h, i):
             slots = slice(i * PIECE * C, (i + 1) * PIECE * C)
-            part = slice(i * PIECE * C // 16, (i + 1) * PIECE * C // 16)
-            nc.vector.tensor_tensor(
-                window[h][:].indirect(offsets[:, part]), result[h][:, slots], gates[:, slots], MULT
-            )
+            nc.gpsimd.tensor_tensor(scaled[h][:, slots], result[h][:, slots], gates[:, slots], MULT)
 
-        def finish(h, cuts):
+        def scatter(h, i0, i1):
+            slots = slice(i0 * PIECE * C, i1 * PIECE * C)
+            part = slice(i0 * PIECE * C // 16, i1 * PIECE * C // 16)
+            nc.vector.tensor_copy(window[h][:].indirect(offsets[:, part]), scaled[h][:, slots])
+
+        def finish(engine, h, cuts):
             for t0, t1 in cuts:
-                nc.vector.tensor_tensor(total[h][:, t0:t1], window[h][:, t0:t1], residual[h][:, t0:t1], ADD)
+                engine.tensor_tensor(total[h][:, t0:t1], window[h][:, t0:t1], residual[h][:, t0:t1], ADD)
                 nc.sync.dma_start(out[h * P : (h + 1) * P, t0:t1], total[h][:, t0:t1])
 
         a = PASSES - 1
-        for i in range(E // PIECE):
-            slots = slice(i * PIECE * C, (i + 1) * PIECE * C)
-            part = slice(i * PIECE * C // 16, (i + 1) * PIECE * C // 16)
+        for i0, i1 in ((0, 1), (1, 3)):
+            slots = slice(i0 * PIECE * C, i1 * PIECE * C)
+            part = slice(i0 * PIECE * C // 16, i1 * PIECE * C // 16)
             nc.vector.tensor_copy(slot_words[a][:, slots], words[a][:].indirect(offsets[:, part]))
             nc.vector.tensor_copy(slot_scales[a][:, slots], scales[a][:].indirect(offsets[:, part]))
-        for h, i in ((0, 0), (0, 1), (1, 0), (0, 2), (1, 1), (1, 2)):
+        for h, i in ((0, 0), (1, 0), (0, 1), (0, 2), (1, 1), (1, 2)):
             multiply(h, i)
             leave_bank(h, i)
-        scatter(0, 0)
-        scatter(0, 1)
-        scatter(1, 0)
-        scatter(0, 2)
-        scatter(1, 1)
-        finish(0, ((0, T),))
-        scatter(1, 2)
-        finish(1, ((0, 768), (768, T)))
+        scatter(0, 0, 1)
+        scatter(1, 0, 1)
+        scatter(0, 1, 3)
+        finish(nc.gpsimd, 0, ((0, 640), (640, T)))
+        scatter(1, 1, 3)
+        finish(nc.vector, 1, ((0, 768), (768, T)))

from contextlib import ExitStack

import concourse.mybir as mybir

K, T, E, C, N = 1024, 1280, 6, 128, 256
S = E * C
P = 128
K_PASS = 512
PASSES = K // K_PASS
HALVES = N // P

FLOPS = 2 * S * K * N
BYTES = 4 * K * T + 8 * N * T + E * K * N // 2 + E * K * N // 32 + 4 * N * E + 4 * S + 2 * P * S // 16

F32 = mybir.dt.float32
BF16 = mybir.dt.bfloat16
I32 = mybir.dt.int32
U32 = mybir.dt.uint32
U16 = mybir.dt.uint16
U8 = mybir.dt.uint8
FP8X4 = mybir.dt.float8_e4m3fn_x4
FP4X4 = mybir.dt.float4_e2m1fn_x4
ADD, MULT = mybir.AluOpType.add, mybir.AluOpType.mult
IDENTITY = mybir.ActivationFunctionType.Identity

CHUNKS = (
    ((0, 512, 184), (512, 512, 184), (1024, 256, 96)),
    ((0, 256, 256), (256, 512, 448), (768, 256, 192), (1024, 256, 96)),
)
PIECE = 2


def interleave(ap_in, ap_out):
    src = ap_in.rearrange("p j (c i) -> p c j i", i=4)
    dst = ap_out.rearrange("p (c i) j -> p c j i", i=4)
    return dst, src


def tile_moe_res_lin_bias_kernel(tc, xT, xr, w_words, w_scales, b, gate, offs, out):
    nc = tc.nc
    with ExitStack() as ctx:
        keep = ctx.enter_context(tc.tile_pool(name="keep", bufs=1))
        psum = ctx.enter_context(tc.psum_pool(name="psum", bufs=1))

        offsets = keep.tile([P, S // 16], U16, name="offsets")

        words = [keep.tile([P, T], U32, name=f"words{a}", align_bytes=64) for a in range(PASSES)]
        scales = [keep.tile([P, T], U8, name=f"scales{a}", align_bytes=64) for a in range(PASSES)]
        slot_words = [keep.tile([P, S], U32, name=f"slot_words{a}", align_bytes=64) for a in range(PASSES)]
        slot_scales = [keep.tile([P, S], U8, name=f"slot_scales{a}", align_bytes=64) for a in range(PASSES)]
        w_code = keep.tile([P, E * PASSES, 2 * N], U8, name="w_code", align_bytes=64)
        w_scale = keep.tile([P, E * PASSES * N], U8, name="w_scale", align_bytes=64)
        window = [keep.tile([P, T], F32, name=f"window{h}") for h in range(HALVES)]
        result = [keep.tile([P, S], F32, name=f"result{h}") for h in range(HALVES)]
        scaled = [keep.tile([P, S], F32, name=f"scaled{h}") for h in range(HALVES)]
        total = [keep.tile([P, T], F32, name=f"total{h}") for h in range(HALVES)]
        residual = [keep.tile([P, T], F32, name=f"residual{h}") for h in range(HALVES)]
        bias = keep.tile([P, HALVES, 8], F32, name="bias")
        gates = keep.tile([P, S], F32, name="gates")

        nc.gpsimd.memset(scales[0][:].bitcast(I32), 0)
        nc.gpsimd.memset(scales[1][:].bitcast(I32), 0)
        nc.gpsimd.memset(w_scale[:].bitcast(I32), 0)
        for h in range(HALVES):
            nc.vector.memset(window[h][:], 0.0)

        raws = []
        for a in range(PASSES):
            row = []
            for i, (t0, width, on_scalar) in enumerate(CHUNKS[a]):
                raw = keep.tile([P, 4, width], F32, name=f"raw{a}_{i}")
                nc.sync.dma_start(
                    raw[:], xT[a * K_PASS : (a + 1) * K_PASS, t0 : t0 + width].rearrange("(p j) w -> p j w", j=4)
                )
                row.append(raw)
                if a == 0 and i == 0:
                    nc.sync.dma_start(offsets[:], offs)
            raws.append(row)

        w_scale_words = w_scale[:].bitcast(I32).rearrange("p (g n) -> p g n", g=E * PASSES)
        scale_rows = w_scales.bitcast(I32).rearrange("e a (q r) n -> r q (e a) n", r=4)
        for r in range(4):
            nc.sync.dma_start(w_scale_words[r:P:32], scale_rows[r])
        code_rows = w_words.rearrange("e a p n -> p (e a) n")
        for e0 in range(0, E, PIECE):
            g = slice(e0 * PASSES, (e0 + PIECE) * PASSES)
            nc.sync.dma_start(w_code[:, g, :], code_rows[:, g, :])
            if e0 == 0:
                nc.sync.dma_start(bias[:, :, 0:E], b.rearrange("(h p) e -> p h e", p=P))
                nc.sync.dma_start(gates[:], gate[0:P, :])
        for h in range(HALVES):
            nc.sync.dma_start(residual[h][:], xr[h * P : (h + 1) * P, :])

        for a in range(PASSES):
            for i, (t0, width, on_scalar) in enumerate(CHUNKS[a]):
                raw = raws[a][i]
                grouped = keep.tile([P, width, 4], BF16, name=f"grouped{a}_{i}", align_bytes=64)
                dst, src = interleave(raw[:, :, 0:on_scalar], grouped[:, 0:on_scalar, :])
                nc.scalar.activation(dst, src, IDENTITY)
                if on_scalar < width:
                    dst, src = interleave(raw[:, :, on_scalar:width], grouped[:, on_scalar:width, :])
                    nc.vector.tensor_copy(dst, src)
                flat = grouped[:].rearrange("p w j -> p (w j)")
                done = 0
                while done < width:
                    cut = max(n for n in (512, 256, 128) if n <= width - done)
                    nc.vector.quantize_mx(
                        out=words[a][:, t0 + done : t0 + done + cut].bitcast(FP8X4),
                        scales=scales[a][:, t0 + done : t0 + done + cut],
                        in_=flat[:, 4 * done : 4 * (done + cut)],
                    )
                    done += cut
            if a == 0:
                nc.vector.tensor_copy(slot_words[a][:], words[a][:].indirect(offsets[:]))
                nc.vector.tensor_copy(slot_scales[a][:], scales[a][:].indirect(offsets[:]))

        banks = [
            [psum.tile([P, PIECE * C], F32, name=f"bank{h}_{i}") for i in range(E // PIECE)] for h in range(HALVES)
        ]

        def multiply(h, i):
            for e in range(i * PIECE, (i + 1) * PIECE):
                slots = slice(e * C, (e + 1) * C)
                local = slice((e - i * PIECE) * C, (e - i * PIECE + 1) * C)
                for a in range(PASSES):
                    g = e * PASSES + a
                    nc.tensor.matmul_mx(
                        out=banks[h][i][:, local],
                        lhsT=w_code[:, g, 2 * P * h : 2 * P * (h + 1)].bitcast(FP4X4),
                        lhsT_scale=w_scale[:, g * N + h * P : g * N + (h + 1) * P],
                        rhs=slot_words[a][:, slots].bitcast(FP8X4),
                        rhs_scale=slot_scales[a][:, slots],
                        start=(a == 0),
                        stop=(a == PASSES - 1),
                    )

        def leave_bank(h, i):
            for e in range(i * PIECE, (i + 1) * PIECE):
                slots = slice(e * C, (e + 1) * C)
                local = slice((e - i * PIECE) * C, (e - i * PIECE + 1) * C)
                nc.scalar.activation(result[h][:, slots], banks[h][i][:, local], IDENTITY, bias=bias[:, h, e : e + 1])

            slots = slice(i * PIECE * C, (i + 1) * PIECE * C)
            nc.gpsimd.tensor_tensor(scaled[h][:, slots], result[h][:, slots], gates[:, slots], MULT)

        def scatter(h, i0, i1):
            slots = slice(i0 * PIECE * C, i1 * PIECE * C)
            part = slice(i0 * PIECE * C // 16, i1 * PIECE * C // 16)
            nc.vector.tensor_copy(window[h][:].indirect(offsets[:, part]), scaled[h][:, slots])

        def finish(engine, h, cuts):
            for t0, t1 in cuts:
                engine.tensor_tensor(total[h][:, t0:t1], window[h][:, t0:t1], residual[h][:, t0:t1], ADD)
                nc.sync.dma_start(out[h * P : (h + 1) * P, t0:t1], total[h][:, t0:t1])

        a = PASSES - 1
        for i0, i1 in ((0, 1), (1, 3)):
            slots = slice(i0 * PIECE * C, i1 * PIECE * C)
            part = slice(i0 * PIECE * C // 16, i1 * PIECE * C // 16)
            nc.vector.tensor_copy(slot_words[a][:, slots], words[a][:].indirect(offsets[:, part]))
            nc.vector.tensor_copy(slot_scales[a][:, slots], scales[a][:].indirect(offsets[:, part]))
        for h, i in ((0, 0), (1, 0), (0, 1), (0, 2), (1, 1), (1, 2)):
            multiply(h, i)
            leave_bank(h, i)
        scatter(0, 0, 1)
        scatter(1, 0, 1)
        scatter(0, 1, 3)
        finish(nc.gpsimd, 0, ((0, 640), (640, T)))
        scatter(1, 1, 3)
        finish(nc.vector, 1, ((0, 768), (768, T)))
